import numpy as np
import ml_dtypes


def mxq(x, axis, fmt="e4m3"):
    dtype, down = {"e4m3": (ml_dtypes.float8_e4m3fn, 7), "e5m2": (ml_dtypes.float8_e5m2, 14)}[fmt]
    v = np.moveaxis(np.asarray(x, np.float32).astype(ml_dtypes.bfloat16).astype(np.float64), axis, -1)
    blocks = v.reshape(v.shape[:-1] + (-1, 32))
    amax = np.abs(blocks).max(-1, keepdims=True)
    byte = np.maximum(np.where(amax > 0, np.frexp(amax)[1] - 1 + 127, 0) - down, 1)
    scale = np.exp2(byte - 127.0)
    codes = (blocks / scale).astype(np.float32).astype(dtype).astype(np.float64)
    return np.moveaxis((codes * scale).reshape(v.shape), -1, axis)


WIDE = False


def mx_kscale(k):
    if not WIDE:
        return np.ones(k)
    levels = np.array([10, -10, 5, -5, 0])
    if k % 512:
        return np.exp2(np.random.permutation(np.resize(levels, k // 32))).repeat(32)
    a = np.empty((k // 512, 16))
    for p in range(k // 512):
        a[p, :8] = np.random.permutation(np.resize(levels, 8))
        for g in range(8):
            far = levels[np.abs(levels - a[p, g]) >= 10]
            a[p, g + 8] = far[np.random.randint(len(far))]
    return np.exp2(a.ravel()).repeat(32)


def f64(x):
    return np.asarray(x).astype(np.float64)


def striped(idx):
    return np.tile(idx.reshape(-1, 16).T, (8, 1)).astype(np.uint16)


def unstriped(offs):
    return offs[:16].T.reshape(-1).astype(np.int64)


def striped8(idx):
    return np.concatenate([x.reshape(-1, 16).T for x in idx]).astype(np.uint16)


def runs(offs, k):
    lists = np.stack([offs[16 * r : 16 * r + 16].T.reshape(-1) for r in range(8)]).astype(np.int64)
    return lists[np.arange(k) % 512 // 64]


def pack_weight(w):
    k, n = w.shape
    w = f64(np.asarray(w, np.float32).astype(ml_dtypes.bfloat16)).reshape(k // 32, 32, n)
    amax = np.abs(w).max(1)
    byte = np.clip(np.where(amax > 0, np.frexp(amax)[1] - 1 + 127 - 7, 1), 1, 254)
    scaled = (w * np.exp2(127.0 - byte)[:, None, :]).reshape(k, n).astype(np.float32)
    words = np.ascontiguousarray(scaled.reshape(k // 512, 128, 4, n).transpose(0, 1, 3, 2)).astype(ml_dtypes.float8_e4m3fn).view(np.uint8)
    return words, np.ascontiguousarray(byte.astype(np.uint8).reshape(k // 512, 16, n))


def unpack_weight(words, scales):
    g, p, n, _ = words.shape
    vals = np.ascontiguousarray(words).view(ml_dtypes.float8_e4m3fn).astype(np.float64) * np.repeat(np.exp2(scales.astype(np.float64) - 127.0), 8, axis=1)[..., None]
    return vals.transpose(0, 1, 3, 2).reshape(g * 512, n)


def sigmoid(v):
    return 1.0 / (1.0 + np.exp(-np.maximum(v, -700.0)))


K, T, S, N, H, C, W = 512, 2048, 512, 512, 512, 512, 256


def setup_inputs():
    n = np.random.standard_normal
    s = mx_kscale(K)[:, None]
    u = mx_kscale(S)
    packed_xT = pack_weight(n((K, T)) * s)
    return {
        "x_words": packed_xT[0],
        "x_scales": packed_xT[1],
        "w1": (n((K, H)) / np.sqrt(K) / s).astype(np.float32),
        "w2": (n((K, H)) / np.sqrt(K) / s).astype(np.float32),
        "gn": (np.random.uniform(0.5, 1.5, (H, 1)) * u[:, None]).astype(np.float32),
        "w3": (n((H, N)) / np.sqrt(H) / u[:, None]).astype(np.float32),
        "gs": (np.random.uniform(0.5, 1.5, (K, 1)) / s).astype(np.float32),
        "offs": striped(np.random.permutation(T)[:S]),
        "two": striped(np.random.permutation(T)[:S]),
        "n1": striped(np.random.permutation(S)),
        "n2": striped(np.random.permutation(S)),
        "n3": striped8(np.stack([np.random.permutation(S) for _ in range(8)])),
        "n4": striped8(np.stack([np.random.permutation(S) for _ in range(8)])),
        "n5": striped8(np.stack([np.random.permutation(S) for _ in range(8)])),
        "cand": striped(np.random.permutation(T)[:C]),
        "n6": striped8(np.stack([np.random.permutation(S)[:W] for _ in range(8)])),
        "n7": striped8(np.stack([np.random.permutation(S)[:W] for _ in range(8)])),
    }


def reference(x_words, x_scales, w1, w2, gn, w3, gs, offs, two, n1, n2, n3, n4, n5, cand, n6, n7):
    x_cand = unpack_weight(x_words, x_scales)[:, unstriped(cand)]
    x_two = unpack_weight(x_words, x_scales)[:, unstriped(two)]
    d = mxq(f64(w2), 0, "e4m3").T @ x_two
    pa = d[np.arange(H)[:, None], runs(n3, H)]
    z2 = f64(gs) * (pa + (sigmoid(d[np.arange(H)[:, None], runs(n4, H)])) * (d[np.arange(H)[:, None], runs(n5, H)] - pa))
    b = 0.0625 * ((x_cand.T @ mxq(z2, 0, "e4m3")))
    xq = unpack_weight(x_words, x_scales)[:, unstriped(offs)]
    y = mxq(f64(w1), 0, "e4m3").T @ xq
    z = f64(gn) * (np.maximum(y * (sigmoid(y[:, unstriped(n1)])), y[:, unstriped(n2)]))
    a = mxq(f64(w3), 0, "e4m3").T @ mxq(z, 0, "e4m3")
    ra = b[np.arange(C)[:, None], runs(n7, C)] - (0.5 * (a[np.arange(N)[:, None], runs(n6, N)]))
    out = a.copy()
    out[np.arange(C)[:, None], runs(n6, C)] = ra
    return out

@@ -1,0 +1,185 @@
+from contextlib import ExitStack
+
+import concourse.mybir as mybir
+
+F32 = mybir.dt.float32
+BF16 = mybir.dt.bfloat16
+I32 = mybir.dt.int32
+U32 = mybir.dt.uint32
+U16 = mybir.dt.uint16
+U8 = mybir.dt.uint8
+FP8X4 = mybir.dt.float8_e4m3fn_x4
+ALU = mybir.AluOpType
+ACT = mybir.ActivationFunctionType
+
+P = 128
+PACK = 4
+T = 2048
+S = 512
+W = 256
+HALF = S // 2
+FLOPS = 4 * 2 * 512 * 512 * 512
+
+
+def tile_picked_tfcdputbgmaxlerp_none_p_kernel(tc, x_words, x_scales, w1, w2, gn, w3, gs, offs, two, n1, n2, n3, n4, n5, cand, n6, n7, out):
+    nc = tc.nc
+    with ExitStack() as ctx:
+        lists = ctx.enter_context(tc.tile_pool(name="lists", bufs=1))
+        keep = ctx.enter_context(tc.tile_pool(name="keep", bufs=1))
+        psum = ctx.enter_context(tc.psum_pool(name="psum", bufs=1))
+
+        def load_list(dram, name):
+            tile = lists.tile(list(dram.shape), U16, name=name)
+            nc.sync.dma_start(tile[:], dram)
+            return tile
+
+        def load_weight(w, name):
+            raw = keep.tile([P, PACK, S], F32, name=name)
+            nc.sync.dma_start(raw[:], w.rearrange("(p j) c -> p j c", j=PACK))
+            return raw
+
+        def load_gain(g, name):
+            tile = keep.tile([P, PACK], F32, name=name)
+            nc.scalar.dma_start(tile[:], g.rearrange("(p t) o -> p (t o)", t=PACK))
+            return tile
+
+        def halves(tile):
+            return [(slice(h * HALF, (h + 1) * HALF), tile[:, h * HALF // 16 : (h + 1) * HALF // 16]) for h in range(2)]
+
+        two_l = load_list(two, "two_l")
+        table_words = keep.tile([P, T], I32, name="table_words")
+        nc.sync.dma_start(table_words[:], x_words[0].rearrange("p n t -> p (n t)").bitcast(I32))
+        table_bytes = keep.tile([P, T], U8, name="table_bytes")
+        nc.vector.memset(table_bytes[:].bitcast(I32), 0)
+        for q in range(4):
+            nc.scalar.dma_start(table_bytes[32 * q : 32 * q + 4, :].bitcast(I32), x_scales[0, 4 * q : 4 * q + 4, :].bitcast(I32))
+        w2_raw = load_weight(w2, "w2_raw")
+        gs_t = load_gain(gs, "gs_t")
+        offs_l = load_list(offs, "offs_l")
+        n3_l = load_list(n3, "n3_l")
+        w1_raw = load_weight(w1, "w1_raw")
+        n5_l = load_list(n5, "n5_l")
+        n4_l = load_list(n4, "n4_l")
+        cand_l = load_list(cand, "cand_l")
+        n1_l = load_list(n1, "n1_l")
+        n2_l = load_list(n2, "n2_l")
+        w3_raw = load_weight(w3, "w3_raw")
+        n6_l = load_list(n6, "n6_l")
+        n7_l = load_list(n7, "n7_l")
+        gn_t = load_gain(gn, "gn_t")
+
+        def pick(list_tile, name, tags, dealt):
+            words = keep.tile([P, S], U32, name=name + "_words", tag=tags[0], align_bytes=64)
+            scales = keep.tile([P, S], U8, name=name + "_scales", tag=tags[1], align_bytes=64)
+            for dst, src in ((words, table_words[:].bitcast(U32)), (scales, table_bytes[:])):
+                view = dst[:].rearrange("p (t m) -> p m t", t=PACK) if dealt else dst[:]
+                nc.vector.tensor_copy(view, src.indirect(list_tile[:]))
+            return words, scales
+
+        def round_weight(raw, name, copy):
+            staged = []
+            for u in range(2):
+                pair = keep.tile([P, 2, P, PACK], BF16, name=f"{name}_pair{u}", tag=f"{name}_stage{u}", align_bytes=64)
+                src = raw[:].rearrange("p j (m t) -> p m j t", t=PACK)[:, :, :, 2 * u : 2 * u + 2]
+                copy(pair[:].rearrange("p t m j -> p m j t"), src)
+                staged.append(pair)
+            return staged
+
+        def quantise_weight(staged, name):
+            words = keep.tile([P, S], U32, name=name + "_words", align_bytes=64)
+            scales = keep.tile([P, S], U8, name=name + "_scales", align_bytes=64)
+            for u, pair in enumerate(staged):
+                cols = slice(u * HALF, (u + 1) * HALF)
+                nc.vector.quantize_mx(words[:, cols].bitcast(FP8X4), scales[:, cols], pair[:].rearrange("p t m j -> p (t m j)"))
+            return words, scales
+
+        def quantise_rows(rounded, name):
+            words = keep.tile([P, S], U32, name=name + "_words", align_bytes=64)
+            scales = keep.tile([P, S], U8, name=name + "_scales", align_bytes=64)
+            nc.vector.quantize_mx(words[:].bitcast(FP8X4), scales[:], rounded[:].rearrange("p c t -> p (c t)"))
+            return words, scales
+
+        def product(stationary, moving, t, tag):
+            bank = psum.tile([P, S], F32, name=f"{tag}{t}", tag=f"{tag}{t}")
+            cols = slice(t * P, (t + 1) * P)
+            nc.tensor.matmul_mx(
+                bank[:],
+                lhsT=stationary[0][:, cols].bitcast(FP8X4),
+                lhsT_scale=stationary[1][:, cols],
+                rhs=moving[0][:].bitcast(FP8X4),
+                rhs_scale=moving[1][:],
+                start=True,
+                stop=True,
+            )
+            return bank
+
+        def by_four(planes):
+            return planes[:].rearrange("p t (c i) -> p c t i", i=4)
+
+        def woven(rounded):
+            return rounded[:].rearrange("p (c i) t -> p c t i", i=4)
+
+        x_two = pick(two_l, "x_two", ("x_two_w", "x_two_s"), False)
+        w2_q = quantise_weight(round_weight(w2_raw, "w2", nc.vector.tensor_copy), "w2")
+        x_offs = pick(offs_l, "x_offs", ("w2_stage0", "w2_stage1"), False)
+        w1_q = quantise_weight(round_weight(w1_raw, "w1", nc.vector.tensor_copy), "w1")
+        x_cand = pick(cand_l, "x_cand", ("w1_stage0", "w1_stage1"), True)
+
+        pa = keep.tile([P, PACK, S], F32, name="pa")
+        step = keep.tile([P, PACK, S], F32, name="step")
+        for t in range(PACK):
+            bank = product(w2_q, x_two, t, "left")
+            d_sig = keep.tile([P, S], F32, name=f"d_sig{t}")
+            d_gain = keep.tile([P, S], F32, name=f"d_gain{t}")
+            diff = keep.tile([P, S], F32, name=f"diff{t}")
+            nc.scalar.activation(d_sig[:], bank[:], ACT.Sigmoid)
+            nc.scalar.activation(d_gain[:], bank[:], ACT.Copy, scale=gs_t[:, t : t + 1])
+            for cols, part in halves(n3_l):
+                nc.scalar.activation(pa[:, t, cols], d_gain[:].indirect(part), ACT.Copy)
+            for cols, part in halves(n5_l):
+                nc.vector.tensor_tensor(diff[:, cols], d_gain[:].indirect(part), pa[:, t, cols], ALU.subtract)
+            for cols, part in halves(n4_l):
+                nc.vector.tensor_tensor(step[:, t, cols], d_sig[:].indirect(part), diff[:, cols], ALU.mult)
+        z2_rounded = keep.tile([P, S, PACK], BF16, name="z2_rounded", align_bytes=64)
+        nc.vector.tensor_tensor(woven(z2_rounded), by_four(pa), by_four(step), ALU.add)
+        z2_q = quantise_rows(z2_rounded, "z2")
+
+        larger = keep.tile([P, PACK, S], F32, name="larger")
+        for t in range(PACK):
+            bank = product(w1_q, x_offs, t, "right")
+            y = keep.tile([P, S], F32, name=f"y{t}")
+            gate = keep.tile([P, S], F32, name=f"gate{t}")
+            other = keep.tile([P, S], F32, name=f"other{t}")
+            gated = keep.tile([P, S], F32, name=f"gated{t}")
+            nc.scalar.copy(y[:], bank[:])
+            for cols, part in halves(n1_l):
+                nc.scalar.activation(gate[:, cols], y[:].indirect(part), ACT.Sigmoid)
+            for cols, part in halves(n2_l):
+                nc.scalar.activation(other[:, cols], y[:].indirect(part), ACT.Copy)
+            nc.vector.tensor_tensor(gated[:], y[:], gate[:], ALU.mult)
+            nc.vector.tensor_tensor(larger[:, t, :], gated[:], other[:], ALU.max)
+        w3_staged = round_weight(w3_raw, "w3", nc.scalar.copy)
+        z_rounded = keep.tile([P, S, PACK], BF16, name="z_rounded", align_bytes=64)
+        gain = gn_t[:].unsqueeze(1).unsqueeze(3).to_broadcast([P, S // 4, PACK, 4])
+        nc.vector.tensor_tensor(woven(z_rounded), by_four(larger), gain, ALU.mult)
+        w3_q = quantise_weight(w3_staged, "w3")
+        z_q = quantise_rows(z_rounded, "z")
+
+        b_picked = []
+        for t in range(PACK):
+            bank = product(x_cand, z2_q, t, "left")
+            b = keep.tile([P, S], F32, name=f"b{t}")
+            nc.scalar.activation(b[:], bank[:], ACT.Copy, scale=0.0625)
+            picked = keep.tile([P, W], F32, name=f"b_picked{t}")
+            nc.scalar.activation(picked[:], b[:].indirect(n7_l[:]), ACT.Copy)
+            b_picked.append(picked)
+
+        out_rows = out.rearrange("(p t) n -> p t n", t=PACK)
+        for t in range(PACK):
+            bank = product(w3_q, z_q, t, "right")
+            a = keep.tile([P, S], F32, name=f"a{t}")
+            nc.scalar.copy(a[:], bank[:])
+            a_picked = keep.tile([P, W], F32, name=f"a_picked{t}")
+            nc.scalar.activation(a_picked[:], a[:].indirect(n6_l[:]), ACT.Copy, scale=-0.5)
+            nc.vector.tensor_tensor(a[:].indirect(n6_l[:]), b_picked[t][:], a_picked[:], ALU.add)
+            nc.sync.dma_start(out_rows[:, t, :], a[:])

@@ -33,81 +33,42 @@ def tile_picked_tfcdputbgmaxlerp_none_p_kernel(tc, x_words, x_scales, w1, w2, gn
             nc.sync.dma_start(tile[:], dram)
             return tile
 
-        def load_weight(w, name):
-            raw = keep.tile([P, PACK, S], F32, name=name)
-            nc.sync.dma_start(raw[:], w.rearrange("(p j) c -> p j c", j=PACK))
+        def load_weight(w_columns, name, tag):
+            raw = keep.tile([P, PACK, w_columns.shape[1]], F32, name=name, tag=tag)
+            nc.sync.dma_start(raw[:], w_columns.rearrange("(p j) c -> p j c", j=PACK))
             return raw
 
         def load_gain(g, name):
             tile = keep.tile([P, PACK], F32, name=name)
-            nc.scalar.dma_start(tile[:], g.rearrange("(p t) o -> p (t o)", t=PACK))
+            nc.sync.dma_start(tile[:], g.rearrange("(p t) o -> p (t o)", t=PACK))
             return tile
 
-        def halves(tile):
-            return [(slice(h * HALF, (h + 1) * HALF), tile[:, h * HALF // 16 : (h + 1) * HALF // 16]) for h in range(2)]
+        def round_weight(staged, raw, copy):
+            copy(staged.rearrange("p t m j -> p m j t"), raw[:].rearrange("p j (m t) -> p m j t", t=PACK))
 
-        two_l = load_list(two, "two_l")
-        table_words = keep.tile([P, T], I32, name="table_words")
-        nc.sync.dma_start(table_words[:], x_words[0].rearrange("p n t -> p (n t)").bitcast(I32))
-        table_bytes = keep.tile([P, T], U8, name="table_bytes")
-        nc.vector.memset(table_bytes[:].bitcast(I32), 0)
-        for q in range(4):
-            nc.scalar.dma_start(table_bytes[32 * q : 32 * q + 4, :].bitcast(I32), x_scales[0, 4 * q : 4 * q + 4, :].bitcast(I32))
-        w2_raw = load_weight(w2, "w2_raw")
-        gs_t = load_gain(gs, "gs_t")
-        offs_l = load_list(offs, "offs_l")
-        n3_l = load_list(n3, "n3_l")
-        w1_raw = load_weight(w1, "w1_raw")
-        n5_l = load_list(n5, "n5_l")
-        n4_l = load_list(n4, "n4_l")
-        cand_l = load_list(cand, "cand_l")
-        n1_l = load_list(n1, "n1_l")
-        n2_l = load_list(n2, "n2_l")
-        w3_raw = load_weight(w3, "w3_raw")
-        n6_l = load_list(n6, "n6_l")
-        n7_l = load_list(n7, "n7_l")
-        gn_t = load_gain(gn, "gn_t")
-
-        def pick(list_tile, name, tags, dealt):
-            words = keep.tile([P, S], U32, name=name + "_words", tag=tags[0], align_bytes=64)
-            scales = keep.tile([P, S], U8, name=name + "_scales", tag=tags[1], align_bytes=64)
-            for dst, src in ((words, table_words[:].bitcast(U32)), (scales, table_bytes[:])):
-                view = dst[:].rearrange("p (t m) -> p m t", t=PACK) if dealt else dst[:]
-                nc.vector.tensor_copy(view, src.indirect(list_tile[:]))
-            return words, scales
-
-        def round_weight(raw, name, copy):
-            staged = []
-            for u in range(2):
-                pair = keep.tile([P, 2, P, PACK], BF16, name=f"{name}_pair{u}", tag=f"{name}_stage{u}", align_bytes=64)
-                src = raw[:].rearrange("p j (m t) -> p m j t", t=PACK)[:, :, :, 2 * u : 2 * u + 2]
-                copy(pair[:].rearrange("p t m j -> p m j t"), src)
-                staged.append(pair)
-            return staged
-
-        def quantise_weight(staged, name):
+        def mx_tiles(name):
             words = keep.tile([P, S], U32, name=name + "_words", align_bytes=64)
             scales = keep.tile([P, S], U8, name=name + "_scales", align_bytes=64)
-            for u, pair in enumerate(staged):
-                cols = slice(u * HALF, (u + 1) * HALF)
-                nc.vector.quantize_mx(words[:, cols].bitcast(FP8X4), scales[:, cols], pair[:].rearrange("p t m j -> p (t m j)"))
             return words, scales
 
-        def quantise_rows(rounded, name):
-            words = keep.tile([P, S], U32, name=name + "_words", align_bytes=64)
-            scales = keep.tile([P, S], U8, name=name + "_scales", align_bytes=64)
-            nc.vector.quantize_mx(words[:].bitcast(FP8X4), scales[:], rounded[:].rearrange("p c t -> p (c t)"))
-            return words, scales
+        def quantise(operand, rounded, cols):
+            nc.vector.quantize_mx(operand[0][:, cols].bitcast(FP8X4), operand[1][:, cols], rounded[:, PACK * cols.start : PACK * cols.stop])
 
-        def product(stationary, moving, t, tag):
-            bank = psum.tile([P, S], F32, name=f"{tag}{t}", tag=f"{tag}{t}")
-            cols = slice(t * P, (t + 1) * P)
+        def pick(dst, table, offsets):
+            nc.vector.tensor_copy(dst, table.indirect(offsets))
+
+        def dealt(tile):
+            return tile[:].rearrange("p (t m) -> p m t", t=PACK)
+
+        def product(stationary, t, moving, cols, tag):
+            bank = psum.tile([P, cols.stop - cols.start], F32, name=tag, tag=tag)
+            rows = slice(t * P, (t + 1) * P)
             nc.tensor.matmul_mx(
                 bank[:],
-                lhsT=stationary[0][:, cols].bitcast(FP8X4),
-                lhsT_scale=stationary[1][:, cols],
-                rhs=moving[0][:].bitcast(FP8X4),
-                rhs_scale=moving[1][:],
+                lhsT=stationary[0][:, rows].bitcast(FP8X4),
+                lhsT_scale=stationary[1][:, rows],
+                rhs=moving[0][:, cols].bitcast(FP8X4),
+                rhs_scale=moving[1][:, cols],
                 start=True,
                 stop=True,
             )
@@ -117,69 +78,135 @@ def tile_picked_tfcdputbgmaxlerp_none_p_kernel(tc, x_words, x_scales, w1, w2, gn
             return planes[:].rearrange("p t (c i) -> p c t i", i=4)
 
         def woven(rounded):
-            return rounded[:].rearrange("p (c i) t -> p c t i", i=4)
+            return rounded[:].rearrange("p (c i t) -> p c t i", i=4, t=PACK)
 
-        x_two = pick(two_l, "x_two", ("x_two_w", "x_two_s"), False)
-        w2_q = quantise_weight(round_weight(w2_raw, "w2", nc.vector.tensor_copy), "w2")
-        x_offs = pick(offs_l, "x_offs", ("w2_stage0", "w2_stage1"), False)
-        w1_q = quantise_weight(round_weight(w1_raw, "w1", nc.vector.tensor_copy), "w1")
-        x_cand = pick(cand_l, "x_cand", ("w1_stage0", "w1_stage1"), True)
+        whole = slice(0, S)
+        halves = (slice(0, HALF), slice(HALF, S))
+
+        table_bytes = keep.tile([P, T], U8, name="table_bytes")
+        nc.vector.memset(table_bytes[:].bitcast(I32), 0)
+        two_l = load_list(two, "two_l")
+        w2_low = load_weight(w2[:, :HALF], "w2_low", "w2_low")
+        offs_l = load_list(offs, "offs_l")
+        for q in range(4):
+            nc.sync.dma_start(table_bytes[32 * q : 32 * q + 4, :].bitcast(I32), x_scales[0, 4 * q : 4 * q + 4, :].bitcast(I32))
+        w2_high = load_weight(w2[:, HALF:], "w2_high", "w2_high")
+        w1_low = load_weight(w1[:, :HALF], "w1_low", "w1_low")
+        cand_l = load_list(cand, "cand_l")
+        table_words = keep.tile([P, T], I32, name="table_words")
+        nc.sync.dma_start(table_words[:], x_words[0].rearrange("p n t -> p (n t)").bitcast(I32))
+        gs_t = load_gain(gs, "gs_t")
+        n3_l = load_list(n3, "n3_l")
+        n5_l = load_list(n5, "n5_l")
+        n4_l = load_list(n4, "n4_l")
+        n1_l = load_list(n1, "n1_l")
+        n2_l = load_list(n2, "n2_l")
+        n6_l = load_list(n6, "n6_l")
+        n7_l = load_list(n7, "n7_l")
+        gn_t = load_gain(gn, "gn_t")
+
+        w2_staged = keep.tile([P, PACK, P, PACK], BF16, name="w2_staged", align_bytes=64)
+        w1_staged = keep.tile([P, PACK, P, PACK], BF16, name="w1_staged", tag="w1_staged", align_bytes=64)
+        round_weight(w2_staged[:, :, : P // 2, :], w2_low, nc.scalar.copy)
+        round_weight(w2_staged[:, :, P // 2 :, :], w2_high, nc.scalar.copy)
+        round_weight(w1_staged[:, :, : P // 2, :], w1_low, nc.scalar.copy)
+        w1_high = load_weight(w1[:, HALF:], "w1_high", "w2_high")
+        w3_raw = load_weight(w3, "w3_raw", "w1_low")
+
+        packed = table_words[:].bitcast(U32)
+        x_two, x_offs, x_cand = mx_tiles("x_two"), mx_tiles("x_offs"), mx_tiles("x_cand")
+        w1_q, w2_q, w3_q = mx_tiles("w1"), mx_tiles("w2"), mx_tiles("w3")
+        pick(x_two[1][:], table_bytes[:], two_l[:])
+        pick(x_offs[1][:], table_bytes[:], offs_l[:])
+        quantise(w2_q, w2_staged[:].rearrange("p t m j -> p (t m j)"), whole)
+        pick(dealt(x_cand[1]), table_bytes[:], cand_l[:])
+        for cols in halves:
+            pick(x_two[0][:, cols], packed, two_l[:, cols.start // 16 : cols.stop // 16])
+        pick(x_offs[0][:], packed, offs_l[:])
+        round_weight(w1_staged[:, :, P // 2 :, :], w1_high, nc.vector.tensor_copy)
+        quantise(w1_q, w1_staged[:].rearrange("p t m j -> p (t m j)"), whole)
+        pick(dealt(x_cand[0]), packed, cand_l[:])
 
         pa = keep.tile([P, PACK, S], F32, name="pa")
         step = keep.tile([P, PACK, S], F32, name="step")
-        for t in range(PACK):
-            bank = product(w2_q, x_two, t, "left")
-            d_sig = keep.tile([P, S], F32, name=f"d_sig{t}")
-            d_gain = keep.tile([P, S], F32, name=f"d_gain{t}")
-            diff = keep.tile([P, S], F32, name=f"diff{t}")
-            nc.scalar.activation(d_sig[:], bank[:], ACT.Sigmoid)
-            nc.scalar.activation(d_gain[:], bank[:], ACT.Copy, scale=gs_t[:, t : t + 1])
-            for cols, part in halves(n3_l):
-                nc.scalar.activation(pa[:, t, cols], d_gain[:].indirect(part), ACT.Copy)
-            for cols, part in halves(n5_l):
-                nc.vector.tensor_tensor(diff[:, cols], d_gain[:].indirect(part), pa[:, t, cols], ALU.subtract)
-            for cols, part in halves(n4_l):
-                nc.vector.tensor_tensor(step[:, t, cols], d_sig[:].indirect(part), diff[:, cols], ALU.mult)
-        z2_rounded = keep.tile([P, S, PACK], BF16, name="z2_rounded", align_bytes=64)
-        nc.vector.tensor_tensor(woven(z2_rounded), by_four(pa), by_four(step), ALU.add)
-        z2_q = quantise_rows(z2_rounded, "z2")
+        diff = keep.tile([P, PACK, S], F32, name="diff", tag="w1_staged", align_bytes=64)
+        d_sig = [keep.tile([P, 2 * S], F32, name=f"d_sig{t}") for t in range(PACK)]
 
-        larger = keep.tile([P, PACK, S], F32, name="larger")
+        def weigh_step(t):
+            nc.vector.tensor_tensor(step[:, t, :], d_sig[t][:].indirect(n4_l[:]), diff[:, t, :], ALU.mult)
+
         for t in range(PACK):
-            bank = product(w1_q, x_offs, t, "right")
-            y = keep.tile([P, S], F32, name=f"y{t}")
-            gate = keep.tile([P, S], F32, name=f"gate{t}")
-            other = keep.tile([P, S], F32, name=f"other{t}")
-            gated = keep.tile([P, S], F32, name=f"gated{t}")
-            nc.scalar.copy(y[:], bank[:])
-            for cols, part in halves(n1_l):
-                nc.scalar.activation(gate[:, cols], y[:].indirect(part), ACT.Sigmoid)
-            for cols, part in halves(n2_l):
-                nc.scalar.activation(other[:, cols], y[:].indirect(part), ACT.Copy)
-            nc.vector.tensor_tensor(gated[:], y[:], gate[:], ALU.mult)
-            nc.vector.tensor_tensor(larger[:, t, :], gated[:], other[:], ALU.max)
-        w3_staged = round_weight(w3_raw, "w3", nc.scalar.copy)
-        z_rounded = keep.tile([P, S, PACK], BF16, name="z_rounded", align_bytes=64)
+            d_gain = keep.tile([P, 2 * S], F32, name=f"d_gain{t}")
+            pieces = zip(halves, ("left0", "right0")) if t == 0 else [(whole, f"left{t}")]
+            for cols, tag in pieces:
+                bank = product(w2_q, t, x_two, cols, tag)
+                nc.scalar.activation(d_sig[t][:, cols], bank[:], ACT.Sigmoid)
+                nc.scalar.activation(d_gain[:, cols], bank[:], ACT.Copy, scale=gs_t[:, t : t + 1])
+            nc.scalar.activation(pa[:, t, :], d_gain[:].indirect(n3_l[:]), ACT.Copy)
+            nc.vector.tensor_tensor(diff[:, t, :], d_gain[:].indirect(n5_l[:]), pa[:, t, :], ALU.subtract)
+            if t > 0:
+                weigh_step(t - 1)
+        weigh_step(PACK - 1)
+        z2_rounded = keep.tile([P, S * PACK], BF16, name="z2_rounded", align_bytes=64)
+        nc.vector.tensor_tensor(woven(z2_rounded), by_four(pa), by_four(step), ALU.add)
+        z2_q = mx_tiles("z2")
+        quantise(z2_q, z2_rounded, whole)
+
+        larger = keep.tile([P, PACK, S], F32, name="larger", tag="larger")
+        other = keep.tile([P, PACK, S], F32, name="other", tag="other")
+        gated = keep.tile([P, PACK, S], F32, name="gated", tag="gated")
+
+        def take_larger(rows):
+            nc.vector.tensor_tensor(larger[:, rows, :], gated[:, rows, :], other[:, rows, :], ALU.max)
+
+        for t in range(PACK):
+            bank = product(w1_q, t, x_offs, whole, f"right{t}")
+            y = keep.tile([P, 2 * S], F32, name=f"y{t}", tag=f"y{t}", align_bytes=64)
+            gate = keep.tile([P, S], F32, name=f"gate{t}", tag=f"gate{t}")
+            nc.scalar.copy(y[:, :S], bank[:])
+            nc.scalar.activation(gate[:], y[:].indirect(n1_l[:]), ACT.Sigmoid)
+            nc.scalar.activation(other[:, t, :], y[:].indirect(n2_l[:]), ACT.Copy)
+            nc.vector.tensor_tensor(gated[:, t, :], y[:, :S], gate[:], ALU.mult)
+            if t == 2:
+                take_larger(slice(0, 2))
+        take_larger(slice(2, 3))
+        take_larger(slice(3, 4))
+        w3_staged = keep.tile([P, PACK, P, PACK], BF16, name="w3_staged", tag="y3", align_bytes=64)
+        round_weight(w3_staged[:], w3_raw, nc.scalar.copy)
+        w3_rounded = w3_staged[:].rearrange("p t m j -> p (t m j)")
+        z_rounded = keep.tile([P, S * PACK], BF16, name="z_rounded", tag="z_rounded", align_bytes=64)
         gain = gn_t[:].unsqueeze(1).unsqueeze(3).to_broadcast([P, S // 4, PACK, 4])
         nc.vector.tensor_tensor(woven(z_rounded), by_four(larger), gain, ALU.mult)
-        w3_q = quantise_weight(w3_staged, "w3")
-        z_q = quantise_rows(z_rounded, "z")
+        z_q = mx_tiles("z")
+        quantise(w3_q, w3_rounded, halves[0])
+        for cols in halves:
+            quantise(z_q, z_rounded, cols)
+        quantise(w3_q, w3_rounded, halves[1])
 
-        b_picked = []
-        for t in range(PACK):
-            bank = product(x_cand, z2_q, t, "left")
-            b = keep.tile([P, S], F32, name=f"b{t}")
+        b_rows = []
+        b_tags = ("gate3", "gated", "other", "larger")
+        for t, tag in enumerate(b_tags):
+            bank = product(x_cand, t, z2_q, whole, f"left{t}")
+            b = keep.tile([P, S], F32, name=f"b{t}", tag=tag)
             nc.scalar.activation(b[:], bank[:], ACT.Copy, scale=0.0625)
-            picked = keep.tile([P, W], F32, name=f"b_picked{t}")
-            nc.scalar.activation(picked[:], b[:].indirect(n7_l[:]), ACT.Copy)
-            b_picked.append(picked)
+            b_rows.append(b)
 
+        b_first = keep.tile([P, W], F32, name="b_first", tag="z_rounded", align_bytes=64)
+        pick(b_first[:], b_rows[0][:], n7_l[:])
         out_rows = out.rearrange("(p t) n -> p t n", t=PACK)
         for t in range(PACK):
-            bank = product(w3_q, z_q, t, "right")
             a = keep.tile([P, S], F32, name=f"a{t}")
-            nc.scalar.copy(a[:], bank[:])
+            pieces = zip(halves, ("right0", "left0")) if t == 0 else [(whole, f"right{t}")]
+            for cols, tag in pieces:
+                bank = product(w3_q, t, z_q, cols, tag)
+                nc.scalar.copy(a[:, cols], bank[:])
             a_picked = keep.tile([P, W], F32, name=f"a_picked{t}")
-            nc.scalar.activation(a_picked[:], a[:].indirect(n6_l[:]), ACT.Copy, scale=-0.5)
-            nc.vector.tensor_tensor(a[:].indirect(n6_l[:]), b_picked[t][:], a_picked[:], ALU.add)
+            if t == 0:
+                b_picked = b_first
+                nc.vector.tensor_scalar(a_picked[:], a[:].indirect(n6_l[:]), -0.5, 0.0, ALU.mult, ALU.add)
+            else:
+                b_picked = keep.tile([P, W], F32, name=f"b_picked{t}", tag=b_tags[t - 1])
+                nc.scalar.activation(a_picked[:], a[:].indirect(n6_l[:]), ACT.Copy, scale=-0.5)
+                nc.scalar.activation(b_picked[:], b_rows[t][:].indirect(n7_l[:]), ACT.Copy)
+            nc.vector.tensor_tensor(a[:].indirect(n6_l[:]), b_picked[:], a_picked[:], ALU.add)
             nc.sync.dma_start(out_rows[:, t, :], a[:])

from contextlib import ExitStack

import concourse.mybir as mybir

F32 = mybir.dt.float32
BF16 = mybir.dt.bfloat16
I32 = mybir.dt.int32
U32 = mybir.dt.uint32
U16 = mybir.dt.uint16
U8 = mybir.dt.uint8
FP8X4 = mybir.dt.float8_e4m3fn_x4
ALU = mybir.AluOpType
ACT = mybir.ActivationFunctionType

P = 128
PACK = 4
T = 2048
S = 512
W = 256
HALF = S // 2
FLOPS = 4 * 2 * 512 * 512 * 512


def tile_picked_tfcdputbgmaxlerp_none_p_kernel(tc, x_words, x_scales, w1, w2, gn, w3, gs, offs, two, n1, n2, n3, n4, n5, cand, n6, n7, out):
    nc = tc.nc
    with ExitStack() as ctx:
        lists = ctx.enter_context(tc.tile_pool(name="lists", bufs=1))
        keep = ctx.enter_context(tc.tile_pool(name="keep", bufs=1))
        psum = ctx.enter_context(tc.psum_pool(name="psum", bufs=1))

        def load_list(dram, name):
            tile = lists.tile(list(dram.shape), U16, name=name)
            nc.sync.dma_start(tile[:], dram)
            return tile

        def load_weight(w_columns, name, tag):
            raw = keep.tile([P, PACK, w_columns.shape[1]], F32, name=name, tag=tag)
            nc.sync.dma_start(raw[:], w_columns.rearrange("(p j) c -> p j c", j=PACK))
            return raw

        def load_gain(g, name):
            tile = keep.tile([P, PACK], F32, name=name)
            nc.sync.dma_start(tile[:], g.rearrange("(p t) o -> p (t o)", t=PACK))
            return tile

        def round_weight(staged, raw, copy):
            copy(staged.rearrange("p t m j -> p m j t"), raw[:].rearrange("p j (m t) -> p m j t", t=PACK))

        def mx_tiles(name):
            words = keep.tile([P, S], U32, name=name + "_words", align_bytes=64)
            scales = keep.tile([P, S], U8, name=name + "_scales", align_bytes=64)
            return words, scales

        def quantise(operand, rounded, cols):
            nc.vector.quantize_mx(operand[0][:, cols].bitcast(FP8X4), operand[1][:, cols], rounded[:, PACK * cols.start : PACK * cols.stop])

        def pick(dst, table, offsets):
            nc.vector.tensor_copy(dst, table.indirect(offsets))

        def dealt(tile):
            return tile[:].rearrange("p (t m) -> p m t", t=PACK)

        def product(stationary, t, moving, cols, tag):
            bank = psum.tile([P, cols.stop - cols.start], F32, name=tag, tag=tag)
            rows = slice(t * P, (t + 1) * P)
            nc.tensor.matmul_mx(
                bank[:],
                lhsT=stationary[0][:, rows].bitcast(FP8X4),
                lhsT_scale=stationary[1][:, rows],
                rhs=moving[0][:, cols].bitcast(FP8X4),
                rhs_scale=moving[1][:, cols],
                start=True,
                stop=True,
            )
            return bank

        def by_four(planes):
            return planes[:].rearrange("p t (c i) -> p c t i", i=4)

        def woven(rounded):
            return rounded[:].rearrange("p (c i t) -> p c t i", i=4, t=PACK)

        whole = slice(0, S)
        halves = (slice(0, HALF), slice(HALF, S))

        table_bytes = keep.tile([P, T], U8, name="table_bytes")
        nc.vector.memset(table_bytes[:].bitcast(I32), 0)
        two_l = load_list(two, "two_l")
        w2_low = load_weight(w2[:, :HALF], "w2_low", "w2_low")
        offs_l = load_list(offs, "offs_l")
        for q in range(4):
            nc.sync.dma_start(table_bytes[32 * q : 32 * q + 4, :].bitcast(I32), x_scales[0, 4 * q : 4 * q + 4, :].bitcast(I32))
        w2_high = load_weight(w2[:, HALF:], "w2_high", "w2_high")
        w1_low = load_weight(w1[:, :HALF], "w1_low", "w1_low")
        cand_l = load_list(cand, "cand_l")
        table_words = keep.tile([P, T], I32, name="table_words")
        nc.sync.dma_start(table_words[:], x_words[0].rearrange("p n t -> p (n t)").bitcast(I32))
        gs_t = load_gain(gs, "gs_t")
        n3_l = load_list(n3, "n3_l")
        n5_l = load_list(n5, "n5_l")
        n4_l = load_list(n4, "n4_l")
        n1_l = load_list(n1, "n1_l")
        n2_l = load_list(n2, "n2_l")
        n6_l = load_list(n6, "n6_l")
        n7_l = load_list(n7, "n7_l")
        gn_t = load_gain(gn, "gn_t")

        w2_staged = keep.tile([P, PACK, P, PACK], BF16, name="w2_staged", align_bytes=64)
        w1_staged = keep.tile([P, PACK, P, PACK], BF16, name="w1_staged", tag="w1_staged", align_bytes=64)
        round_weight(w2_staged[:, :, : P // 2, :], w2_low, nc.scalar.copy)
        round_weight(w2_staged[:, :, P // 2 :, :], w2_high, nc.scalar.copy)
        round_weight(w1_staged[:, :, : P // 2, :], w1_low, nc.scalar.copy)
        w1_high = load_weight(w1[:, HALF:], "w1_high", "w2_high")
        w3_raw = load_weight(w3, "w3_raw", "w1_low")

        packed = table_words[:].bitcast(U32)
        x_two, x_offs, x_cand = mx_tiles("x_two"), mx_tiles("x_offs"), mx_tiles("x_cand")
        w1_q, w2_q, w3_q = mx_tiles("w1"), mx_tiles("w2"), mx_tiles("w3")
        pick(x_two[1][:], table_bytes[:], two_l[:])
        pick(x_offs[1][:], table_bytes[:], offs_l[:])
        quantise(w2_q, w2_staged[:].rearrange("p t m j -> p (t m j)"), whole)
        pick(dealt(x_cand[1]), table_bytes[:], cand_l[:])
        for cols in halves:
            pick(x_two[0][:, cols], packed, two_l[:, cols.start // 16 : cols.stop // 16])
        pick(x_offs[0][:], packed, offs_l[:])
        round_weight(w1_staged[:, :, P // 2 :, :], w1_high, nc.vector.tensor_copy)
        quantise(w1_q, w1_staged[:].rearrange("p t m j -> p (t m j)"), whole)
        pick(dealt(x_cand[0]), packed, cand_l[:])

        pa = keep.tile([P, PACK, S], F32, name="pa")
        step = keep.tile([P, PACK, S], F32, name="step")
        diff = keep.tile([P, PACK, S], F32, name="diff", tag="w1_staged", align_bytes=64)
        d_sig = [keep.tile([P, 2 * S], F32, name=f"d_sig{t}") for t in range(PACK)]

        def weigh_step(t):
            nc.vector.tensor_tensor(step[:, t, :], d_sig[t][:].indirect(n4_l[:]), diff[:, t, :], ALU.mult)

        for t in range(PACK):
            d_gain = keep.tile([P, 2 * S], F32, name=f"d_gain{t}")
            pieces = zip(halves, ("left0", "right0")) if t == 0 else [(whole, f"left{t}")]
            for cols, tag in pieces:
                bank = product(w2_q, t, x_two, cols, tag)
                nc.scalar.activation(d_sig[t][:, cols], bank[:], ACT.Sigmoid)
                nc.scalar.activation(d_gain[:, cols], bank[:], ACT.Copy, scale=gs_t[:, t : t + 1])
            nc.scalar.activation(pa[:, t, :], d_gain[:].indirect(n3_l[:]), ACT.Copy)
            nc.vector.tensor_tensor(diff[:, t, :], d_gain[:].indirect(n5_l[:]), pa[:, t, :], ALU.subtract)
            if t > 0:
                weigh_step(t - 1)
        weigh_step(PACK - 1)
        z2_rounded = keep.tile([P, S * PACK], BF16, name="z2_rounded", align_bytes=64)
        nc.vector.tensor_tensor(woven(z2_rounded), by_four(pa), by_four(step), ALU.add)
        z2_q = mx_tiles("z2")
        quantise(z2_q, z2_rounded, whole)

        larger = keep.tile([P, PACK, S], F32, name="larger", tag="larger")
        other = keep.tile([P, PACK, S], F32, name="other", tag="other")
        gated = keep.tile([P, PACK, S], F32, name="gated", tag="gated")

        def take_larger(rows):
            nc.vector.tensor_tensor(larger[:, rows, :], gated[:, rows, :], other[:, rows, :], ALU.max)

        for t in range(PACK):
            bank = product(w1_q, t, x_offs, whole, f"right{t}")
            y = keep.tile([P, 2 * S], F32, name=f"y{t}", tag=f"y{t}", align_bytes=64)
            gate = keep.tile([P, S], F32, name=f"gate{t}", tag=f"gate{t}")
            nc.scalar.copy(y[:, :S], bank[:])
            nc.scalar.activation(gate[:], y[:].indirect(n1_l[:]), ACT.Sigmoid)
            nc.scalar.activation(other[:, t, :], y[:].indirect(n2_l[:]), ACT.Copy)
            nc.vector.tensor_tensor(gated[:, t, :], y[:, :S], gate[:], ALU.mult)
            if t == 2:
                take_larger(slice(0, 2))
        take_larger(slice(2, 3))
        take_larger(slice(3, 4))
        w3_staged = keep.tile([P, PACK, P, PACK], BF16, name="w3_staged", tag="y3", align_bytes=64)
        round_weight(w3_staged[:], w3_raw, nc.scalar.copy)
        w3_rounded = w3_staged[:].rearrange("p t m j -> p (t m j)")
        z_rounded = keep.tile([P, S * PACK], BF16, name="z_rounded", tag="z_rounded", align_bytes=64)
        gain = gn_t[:].unsqueeze(1).unsqueeze(3).to_broadcast([P, S // 4, PACK, 4])
        nc.vector.tensor_tensor(woven(z_rounded), by_four(larger), gain, ALU.mult)
        z_q = mx_tiles("z")
        quantise(w3_q, w3_rounded, halves[0])
        for cols in halves:
            quantise(z_q, z_rounded, cols)
        quantise(w3_q, w3_rounded, halves[1])

        b_rows = []
        b_tags = ("gate3", "gated", "other", "larger")
        for t, tag in enumerate(b_tags):
            bank = product(x_cand, t, z2_q, whole, f"left{t}")
            b = keep.tile([P, S], F32, name=f"b{t}", tag=tag)
            nc.scalar.activation(b[:], bank[:], ACT.Copy, scale=0.0625)
            b_rows.append(b)

        b_first = keep.tile([P, W], F32, name="b_first", tag="z_rounded", align_bytes=64)
        pick(b_first[:], b_rows[0][:], n7_l[:])
        out_rows = out.rearrange("(p t) n -> p t n", t=PACK)
        for t in range(PACK):
            a = keep.tile([P, S], F32, name=f"a{t}")
            pieces = zip(halves, ("right0", "left0")) if t == 0 else [(whole, f"right{t}")]
            for cols, tag in pieces:
                bank = product(w3_q, t, z_q, cols, tag)
                nc.scalar.copy(a[:, cols], bank[:])
            a_picked = keep.tile([P, W], F32, name=f"a_picked{t}")
            if t == 0:
                b_picked = b_first
                nc.vector.tensor_scalar(a_picked[:], a[:].indirect(n6_l[:]), -0.5, 0.0, ALU.mult, ALU.add)
            else:
                b_picked = keep.tile([P, W], F32, name=f"b_picked{t}", tag=b_tags[t - 1])
                nc.scalar.activation(a_picked[:], a[:].indirect(n6_l[:]), ACT.Copy, scale=-0.5)
                nc.scalar.activation(b_picked[:], b_rows[t][:].indirect(n7_l[:]), ACT.Copy)
            nc.vector.tensor_tensor(a[:].indirect(n6_l[:]), b_picked[:], a_picked[:], ALU.add)
            nc.sync.dma_start(out_rows[:, t, :], a[:])
